import numpy as np
import ml_dtypes


def mxq(x, axis, fmt="e4m3"):
    dtype, down = {"e4m3": (ml_dtypes.float8_e4m3fn, 7), "e5m2": (ml_dtypes.float8_e5m2, 14)}[fmt]
    v = np.moveaxis(np.asarray(x, np.float32).astype(ml_dtypes.bfloat16).astype(np.float64), axis, -1)
    blocks = v.reshape(v.shape[:-1] + (-1, 32))
    amax = np.abs(blocks).max(-1, keepdims=True)
    byte = np.maximum(np.where(amax > 0, np.frexp(amax)[1] - 1 + 127, 0) - down, 1)
    scale = np.exp2(byte - 127.0)
    codes = (blocks / scale).astype(np.float32).astype(dtype).astype(np.float64)
    return np.moveaxis((codes * scale).reshape(v.shape), -1, axis)


WIDE = False


def mx_kscale(k):
    if not WIDE:
        return np.ones(k)
    levels = np.array([30, -30])
    if k % 512:
        return np.exp2(np.random.permutation(np.resize(levels, k // 32))).repeat(32)
    a = np.empty((k // 512, 16))
    for p in range(k // 512):
        a[p, :8] = np.random.permutation(np.resize(levels, 8))
        for g in range(8):
            far = levels[np.abs(levels - a[p, g]) >= 10]
            a[p, g + 8] = far[np.random.randint(len(far))]
    return np.exp2(a.ravel()).repeat(32)


BF16 = ml_dtypes.bfloat16


def bf(x):
    return np.asarray(x, np.float32).astype(BF16)


def f64(x):
    return np.asarray(x).astype(np.float64)


E2M1 = np.array([0.0, 0.5, 1.0, 1.5, 2.0, 3.0, 4.0, 6.0, -0.0, -0.5, -1.0, -1.5, -2.0, -3.0, -4.0, -6.0])


def pack_weight(w, fmt):
    k, n = w.shape
    w = f64(bf(w)).reshape(k // 32, 32, n)
    amax = np.abs(w).max(1)
    if fmt == "e4m3":
        byte = np.frexp(amax)[1] - 1 + 127 - 7
    else:
        mant, ex = np.frexp(amax / 6.0)
        byte = np.where(mant > 0.5, ex, ex - 1) + 127
    byte = np.clip(np.where(amax > 0, byte, 1), 1, 254)
    scaled = (w * np.exp2(127.0 - byte)[:, None, :]).reshape(k, n).astype(np.float32)
    by_word = np.ascontiguousarray(scaled.reshape(k // 512, 128, 4, n).transpose(0, 1, 3, 2))
    if fmt == "e4m3":
        words = by_word.astype(ml_dtypes.float8_e4m3fn).view(np.uint8)
    else:
        c = by_word.astype(ml_dtypes.float4_e2m1fn).view(np.uint8) & 0xF
        words = c[..., 0::2] | (c[..., 1::2] << 4)
    return np.ascontiguousarray(words), np.ascontiguousarray(byte.astype(np.uint8).reshape(k // 512, 16, n))


def unpack_weight(words, scales, fmt):
    g, p, n, _ = words.shape
    if fmt == "e4m3":
        vals = np.ascontiguousarray(words).view(ml_dtypes.float8_e4m3fn).astype(np.float64)
    else:
        nib = np.empty((g, p, n, 4), np.uint8)
        nib[..., 0::2] = words & 0xF
        nib[..., 1::2] = words >> 4
        vals = E2M1[nib]
    vals = vals * np.repeat(np.exp2(scales.astype(np.float64) - 127.0), 8, axis=1)[..., None]
    return vals.transpose(0, 1, 3, 2).reshape(g * 512, n)
def pack4(w):
    words, scales = pack_weight(w, "e2m1")
    return words.reshape(words.shape[0], 128, -1), scales


def unpack4(words, scales):
    return unpack_weight(words.reshape(words.shape[0], 128, -1, 2), scales, "e2m1")


T, O, F, C = 1024, 2048, 1024, 1024


def setup_inputs():
    s, u = mx_kscale(O), mx_kscale(T)
    v = np.random.standard_normal((O, F)) / np.sqrt(O) / s[:, None]
    v_words, v_scales = pack4(v)
    return {"delta": bf(0.2 * np.random.standard_normal((T, O)) * s / u[:, None]),
            "v_words": v_words,
            "v_scales": v_scales,
            "gain": bf(1 + 0.1 * np.random.standard_normal(F)),
            "x": bf(np.random.standard_normal((T, C)) * u[:, None]),
            "lo": bf(-(0.8 + 0.4 * np.random.random(T)) * u),
            "hi": bf((1.2 + 0.4 * np.random.random(T)) * u),
            "w": bf(np.random.standard_normal((C, F)) / np.sqrt(C)),
            "r": bf((1.0 + 0.5 * np.random.random(F)) / np.sqrt(C))}


def reference(delta, v_words, v_scales, gain, x, lo, hi, w, r):
    back = mxq(f64(delta), 1, "e4m3") @ unpack4(v_words, v_scales)
    e = back * f64(gain)
    xc = np.minimum(np.maximum(f64(x), f64(lo)[:, None]), f64(hi)[:, None])
    dw = mxq(xc, 0, "e4m3").T @ mxq(e, 0, "e5m2")
    inside = np.abs(f64(w)) <= f64(r)
    return dw * inside

@@ -1,0 +1,290 @@
+from contextlib import ExitStack
+
+import concourse.mybir as mybir
+from concourse.masks import make_identity
+
+T, O, F, C = 1024, 2048, 1024, 1024
+FLOPS = 2 * T * O * F + 2 * T * F * C
+
+F32 = mybir.dt.float32
+BF16 = mybir.dt.bfloat16
+I32 = mybir.dt.int32
+U32 = mybir.dt.uint32
+U8 = mybir.dt.uint8
+E4M3 = mybir.dt.float8_e4m3fn_x4
+E5M2 = mybir.dt.float8_e5m2_x4
+E2M1 = mybir.dt.float4_e2m1fn_x4
+OP = mybir.AluOpType
+ACT = mybir.ActivationFunctionType
+
+P = 128
+KG = O // 512
+TG = T // 512
+
+
+def tile_straight_through_weight_gradient_s9_kernel(
+    tc, delta, v_words, v_scales, gain, x, lo, hi, w, r, out
+):
+    nc = tc.nc
+    with ExitStack() as ctx:
+        keep = ctx.enter_context(tc.tile_pool(name="keep", bufs=1))
+        stage = ctx.enter_context(tc.tile_pool(name="stage", bufs=3))
+        outs = ctx.enter_context(tc.tile_pool(name="outs", bufs=8))
+        psum = ctx.enter_context(tc.psum_pool(name="psum", bufs=1))
+        ctx.enter_context(tc.manual_schedule())
+
+        vs = keep.tile([P, KG, F], U8, align_bytes=64)
+        nc.vector.memset(vs[:].rearrange("p g n -> p (g n)").bitcast(I32), 0)
+        warm = keep.tile([P, 1], F32)
+        nc.vector.memset(warm[:], 0.0)
+        warm2 = keep.tile([P, 1], F32)
+        nc.scalar.activation(out=warm2[:], in_=warm[:], func=ACT.Abs)
+        ident = keep.tile([P, P], F32)
+        make_identity(nc, ident[:])
+        lo_sb = keep.tile([P, TG, 4], BF16)
+        hi_sb = keep.tile([P, TG, 4], BF16)
+        nc.gpsimd.dma_start(out=lo_sb[:], in_=lo.rearrange("(g p j) -> p g j", p=P, j=4))
+        nc.gpsimd.dma_start(out=hi_sb[:], in_=hi.rearrange("(g p j) -> p g j", p=P, j=4))
+
+        delta_v = delta.rearrange("(g m t) k -> g t m k", m=P, t=4)
+        x_v = x.rearrange("(g p j) c -> g p j c", p=P, j=4)
+        w_v = w.rearrange("(ct p) f -> p ct f", p=P)
+        vw_v = v_words.rearrange("g p b -> p g b")
+        vs_v = v_scales.rearrange("g q n -> q g n").bitcast(I32)
+
+        d_sb = [keep.tile([P, O], BF16, name=f"d_sb{i}") for i in range(8)]
+        vw = [keep.tile([P, KG, F], U8, name=f"vw{h}", align_bytes=64) for h in range(2)]
+        gain_bc = keep.tile([P, F], BF16)
+        r_bc = keep.tile([P, F], BF16)
+        x_sb = [keep.tile([P, 4, C], BF16, name=f"x_sb{g}") for g in range(TG)]
+        w_sb = keep.tile([P, 8, F], BF16)
+
+        def load_d(i, pieces=1):
+            n = O // pieces
+            for k in range(pieces):
+                nc.sync.dma_start(
+                    out=d_sb[i][:, k * n : (k + 1) * n],
+                    in_=delta_v[i // 4, i % 4, :, k * n : (k + 1) * n],
+                )
+
+        def load_vs():
+            for q in range(4):
+                nc.sync.dma_start(
+                    out=vs[32 * q : 32 * q + 4, :, :].bitcast(I32), in_=vs_v[4 * q : 4 * q + 4, :, :]
+                )
+
+        def load_vw(h):
+            nc.sync.dma_start(out=vw[h][:], in_=vw_v[:, :, h * F : (h + 1) * F])
+
+        def load_x(g):
+            for a in range(2):
+                nc.sync.dma_start(out=x_sb[g][:, 2 * a : 2 * a + 2, :], in_=x_v[g, :, 2 * a : 2 * a + 2, :])
+
+        def load_w(a):
+            nc.sync.dma_start(out=w_sb[:, 2 * a : 2 * a + 2, :], in_=w_v[:, 2 * a : 2 * a + 2, :])
+
+        load_d(0, 2)
+        load_d(1)
+        load_d(2)
+        load_d(3)
+        load_vs()
+        load_vw(0)
+        load_d(4)
+        load_d(5)
+        nc.sync.dma_start(out=gain_bc[:], in_=gain.partition_broadcast(P))
+        load_x(0)
+        load_vw(1)
+        load_d(6)
+        load_d(7)
+        load_x(1)
+        load_w(0)
+        nc.sync.dma_start(out=r_bc[:], in_=r.partition_broadcast(P))
+        load_w(1)
+        load_w(2)
+        load_w(3)
+
+        d_codes = [keep.tile([P, 512], U32, name=f"d_codes{i}", align_bytes=64) for i in range(8)]
+        d_scales = [keep.tile([P, 512], U8, name=f"d_scales{i}", align_bytes=64) for i in range(8)]
+        x_grp = [keep.tile([P, C, 4], BF16, name=f"x_grp{g}", align_bytes=64) for g in range(TG)]
+        x_codes = [keep.tile([P, C], U32, name=f"x_codes{g}", align_bytes=64) for g in range(TG)]
+        x_scales = [keep.tile([P, C], U8, name=f"x_scales{g}", align_bytes=64) for g in range(TG)]
+        e_grp = [keep.tile([P, F, 4], BF16, name=f"e_grp{g}", align_bytes=64) for g in range(TG)]
+        e_codes = [keep.tile([P, F], U32, name=f"e_codes{g}", align_bytes=64) for g in range(TG)]
+        e_scales = [keep.tile([P, F], U8, name=f"e_scales{g}", align_bytes=64) for g in range(TG)]
+        mask = keep.tile([P, 8, F], BF16)
+
+        def bank(n):
+            return psum.tile([P, 512], F32, name=f"bank{n}", tag=f"bank{n}")
+
+        tbanks = {}
+        mbanks = {}
+        d_grp = {}
+
+        def T_(i):
+            words = d_sb[i][:].bitcast(F32)
+            for b in range(2):
+                ps = bank((i % 2) * 2 + b)
+                tbanks[(i, b)] = ps
+                for s in range(2):
+                    for u in range(2):
+                        k0 = 256 * (2 * b + s)
+                        q = 2 * s + u
+                        nc.tensor.transpose(
+                            ps[:, q * P : (q + 1) * P], words[:, k0 + u : k0 + 256 : 2], ident[:]
+                        )
+
+        def C_(i):
+            grp = stage.tile([P, KG, P, 4], BF16, name="d_grp", align_bytes=64)
+            d_grp[i] = grp
+            gw = grp[:].rearrange("p g r t -> p (g r t)").bitcast(F32)
+            gw = gw.rearrange("p (g r u) -> p g r u", g=KG, u=2)
+            for b in range(2):
+                nc.scalar.copy(
+                    out=gw[:, 2 * b : 2 * b + 2, :, :],
+                    in_=tbanks[(i, b)][:].rearrange("p (s u r) -> p s r u", s=2, u=2),
+                )
+
+        def Q_(i):
+            nc.vector.quantize_mx(
+                out=d_codes[i][:].bitcast(E4M3),
+                scales=d_scales[i][:],
+                in_=d_grp[i][:].rearrange("p g r t -> p (g r t)"),
+            )
+
+        def mx1(i, fc, ps):
+            t = i % 4
+            for g in range(KG):
+                nc.tensor.matmul_mx(
+                    out=ps[:, t * P : (t + 1) * P],
+                    lhsT=d_codes[i][:, g * P : (g + 1) * P].bitcast(E4M3),
+                    lhsT_scale=d_scales[i][:, g * P : (g + 1) * P],
+                    rhs=vw[fc // 4][:, g, 256 * (fc % 4) : 256 * (fc % 4) + 256].bitcast(E2M1),
+                    rhs_scale=vs[:, g, P * fc : P * fc + P],
+                    start=(g == 0),
+                    stop=(g == KG - 1),
+                )
+
+        def M_(i):
+            for fc in range(4):
+                if i % 4 == 0:
+                    mbanks[(i // 4, fc)] = bank(4 + fc)
+                mx1(i, fc, mbanks[(i // 4, fc)])
+
+        def B_(G, fc):
+            mbanks[(G, fc)] = bank(4 + fc % 4)
+            for t in range(4):
+                mx1(4 * G + t, fc, mbanks[(G, fc)])
+
+        def G_(G, fc):
+            nc.vector.tensor_tensor(
+                out=e_grp[G][:, fc * P : (fc + 1) * P, :],
+                in0=mbanks[(G, fc)][:].rearrange("p (t n) -> p n t", t=4),
+                in1=gain_bc[:, fc * P : (fc + 1) * P].unsqueeze(2).to_broadcast([P, P, 4]),
+                op=OP.mult,
+            )
+
+        def QE_(G, f0, n):
+            nc.vector.quantize_mx(
+                out=e_codes[G][:, f0 : f0 + n].bitcast(E5M2),
+                scales=e_scales[G][:, f0 : f0 + n],
+                in_=e_grp[G][:, f0 : f0 + n, :].rearrange("p n t -> p (n t)"),
+            )
+
+        def CL_(G, j):
+            nc.vector.tensor_scalar(
+                out=x_sb[G][:, j, :],
+                in0=x_sb[G][:, j, :],
+                scalar1=lo_sb[:, G, j : j + 1],
+                scalar2=hi_sb[:, G, j : j + 1],
+                op0=OP.max,
+                op1=OP.min,
+            )
+
+        def I_(G, c0, n, eng):
+            o = x_grp[G][:, c0 : c0 + n, :]
+            i = x_sb[G][:, :, c0 : c0 + n].rearrange("p j c -> p c j")
+            if eng == "s":
+                nc.scalar.copy(out=o, in_=i)
+            else:
+                nc.vector.tensor_copy(out=o, in_=i)
+
+        def QX_(G, c0, n):
+            nc.vector.quantize_mx(
+                out=x_codes[G][:, c0 : c0 + n].bitcast(E4M3),
+                scales=x_scales[G][:, c0 : c0 + n],
+                in_=x_grp[G][:, c0 : c0 + n, :].rearrange("p c j -> p (c j)"),
+            )
+
+        def A_(ct):
+            nc.scalar.activation(out=w_sb[:, ct, :], in_=w_sb[:, ct, :], func=ACT.Abs)
+
+        def K_(ct):
+            nc.vector.tensor_tensor(out=mask[:, ct, :], in0=w_sb[:, ct, :], in1=r_bc[:], op=OP.is_le)
+
+        obanks = {}
+        counter = {"n": 0}
+
+        def S2_(ct, h):
+            ps = bank(counter["n"] % 8)
+            counter["n"] += 1
+            obanks[(ct, h)] = ps
+            for G in range(TG):
+                nc.tensor.matmul_mx(
+                    out=ps[:],
+                    lhsT=x_codes[G][:, ct * P : (ct + 1) * P].bitcast(E4M3),
+                    lhsT_scale=x_scales[G][:, ct * P : (ct + 1) * P],
+                    rhs=e_codes[G][:, h * 512 : (h + 1) * 512].bitcast(E5M2),
+                    rhs_scale=e_scales[G][:, h * 512 : (h + 1) * 512],
+                    start=(G == 0),
+                    stop=(G == TG - 1),
+                )
+
+        def O_(ct, h, eng="v"):
+            res = outs.tile([P, 512], F32, name="res")
+            m = mask[:, ct, h * 512 : (h + 1) * 512]
+            if eng == "v":
+                nc.vector.tensor_tensor(out=res[:], in0=obanks[(ct, h)][:], in1=m, op=OP.mult)
+            else:
+                nc.scalar.copy(out=res[:], in_=obanks[(ct, h)][:])
+                nc.gpsimd.tensor_tensor(out=res[:], in0=res[:], in1=m, op=OP.mult)
+            nc.sync.dma_start(out=out[ct * P : (ct + 1) * P, h * 512 : (h + 1) * 512], in_=res[:])
+
+        T_(0); C_(0); T_(1); C_(1); Q_(0); T_(2); C_(2); Q_(1); T_(3); C_(3); Q_(2)
+        M_(0); Q_(3)
+        M_(1); T_(4); C_(4)
+        T_(5); C_(5); Q_(4)
+        M_(2); CL_(0, 0); CL_(0, 1); CL_(0, 2); CL_(0, 3); Q_(5)
+        I_(0, 0, 256, "s"); I_(0, 256, 256, "s")
+        M_(3); G_(0, 0); G_(0, 1); G_(0, 2); QE_(0, 0, 256); G_(0, 3)
+        B_(0, 4); I_(0, 512, 256, "s"); QE_(0, 256, 256)
+        B_(0, 5); G_(0, 4)
+        T_(6); C_(6); T_(7); C_(7); G_(0, 5); Q_(6); QE_(0, 512, 256)
+        I_(0, 768, 256, "s")
+        B_(0, 6); CL_(1, 0); CL_(1, 1); CL_(1, 2); CL_(1, 3); Q_(7)
+        I_(1, 0, 256, "s"); I_(1, 256, 256, "s")
+        B_(0, 7); G_(0, 6); QX_(0, 0, 512); G_(0, 7); QX_(0, 512, 512)
+        I_(1, 512, 256, "s"); I_(1, 768, 256, "s")
+        QE_(0, 768, 256)
+        for fc in range(8):
+            B_(1, fc)
+            A_(fc)
+            if fc > 0:
+                G_(1, fc - 1)
+            if fc == 3:
+                QX_(1, 0, 512)
+            if fc == 5:
+                QX_(1, 512, 512)
+            if fc in (3, 5, 7):
+                QE_(1, 128 * (fc - 3), 256)
+            if fc > 3:
+                K_(fc - 4)
+        G_(1, 7)
+        K_(4)
+        QE_(1, 768, 256)
+        order = [(0, 0), (1, 0), (2, 0), (0, 1), (1, 1), (2, 1), (3, 0), (3, 1), (4, 0), (4, 1), (5, 0), (5, 1),
+                 (6, 0), (6, 1), (7, 0), (7, 1)]
+        for n, (ct, h) in enumerate(order):
+            S2_(ct, h)
+            if n in (2, 5, 8):
+                K_(n // 3 + 5)
+            O_(ct, h, "s" if n in (4, 7, 10, 12) else "v")

@@ -29,10 +29,12 @@ def tile_straight_through_weight_gradient_s9_kernel(
     with ExitStack() as ctx:
         keep = ctx.enter_context(tc.tile_pool(name="keep", bufs=1))
         stage = ctx.enter_context(tc.tile_pool(name="stage", bufs=3))
-        outs = ctx.enter_context(tc.tile_pool(name="outs", bufs=8))
+        outs = ctx.enter_context(tc.tile_pool(name="outs", bufs=16))
         psum = ctx.enter_context(tc.psum_pool(name="psum", bufs=1))
         ctx.enter_context(tc.manual_schedule())
 
+        vrow = keep.tile([P, P], BF16)
+        nc.vector.memset(vrow[:], 0.0)
         vs = keep.tile([P, KG, F], U8, align_bytes=64)
         nc.vector.memset(vs[:].rearrange("p g n -> p (g n)").bitcast(I32), 0)
         warm = keep.tile([P, 1], F32)
@@ -41,6 +43,8 @@ def tile_straight_through_weight_gradient_s9_kernel(
         nc.scalar.activation(out=warm2[:], in_=warm[:], func=ACT.Abs)
         ident = keep.tile([P, P], F32)
         make_identity(nc, ident[:])
+        ident_bf = keep.tile([P, P], BF16)
+        nc.vector.tensor_copy(out=ident_bf[:], in_=ident[:])
         lo_sb = keep.tile([P, TG, 4], BF16)
         hi_sb = keep.tile([P, TG, 4], BF16)
         nc.gpsimd.dma_start(out=lo_sb[:], in_=lo.rearrange("(g p j) -> p g j", p=P, j=4))
@@ -85,23 +89,21 @@ def tile_straight_through_weight_gradient_s9_kernel(
 
         load_d(0, 2)
         load_d(1)
+        nc.sync.dma_start(out=vrow[0:8, :], in_=gain.rearrange("(c p) -> c p", p=P))
         load_d(2)
-        load_d(3)
         load_vs()
+        load_d(3)
         load_vw(0)
+        load_x(0)
         load_d(4)
         load_d(5)
-        nc.sync.dma_start(out=gain_bc[:], in_=gain.partition_broadcast(P))
-        load_x(0)
         load_vw(1)
+        load_x(1)
         load_d(6)
         load_d(7)
-        load_x(1)
-        load_w(0)
+        for a in range(4):
+            load_w(a)
         nc.sync.dma_start(out=r_bc[:], in_=r.partition_broadcast(P))
-        load_w(1)
-        load_w(2)
-        load_w(3)
 
         d_codes = [keep.tile([P, 512], U32, name=f"d_codes{i}", align_bytes=64) for i in range(8)]
         d_scales = [keep.tile([P, 512], U8, name=f"d_scales{i}", align_bytes=64) for i in range(8)]
@@ -132,6 +134,21 @@ def tile_straight_through_weight_gradient_s9_kernel(
                         nc.tensor.transpose(
                             ps[:, q * P : (q + 1) * P], words[:, k0 + u : k0 + 256 : 2], ident[:]
                         )
+
+        v_cols = keep.tile([P, 8], BF16)
+
+        def VT_():
+            ps = psum.tile([P, 1024], BF16, name="bank4v", tag="bank4")
+            nc.tensor.transpose(ps[:, 0:P], vrow[:], ident_bf[:])
+            nc.vector.tensor_copy(out=v_cols[:], in_=ps[:, 0:8])
+
+        def VB_(n, dst):
+            ps = psum.tile([P, 1024], BF16, name=f"bank{5 + n}v", tag=f"bank{5 + n}")
+            for c in range(8):
+                nc.tensor.transpose(
+                    ps[:, c * P : (c + 1) * P], v_cols[:, 8 * n + c : 8 * n + c + 1].to_broadcast([P, P]), ident_bf[:]
+                )
+            nc.scalar.copy(out=dst[:], in_=ps[:])
 
         def C_(i):
             grp = stage.tile([P, KG, P, 4], BF16, name="d_grp", align_bytes=64)
@@ -169,6 +186,10 @@ def tile_straight_through_weight_gradient_s9_kernel(
                 if i % 4 == 0:
                     mbanks[(i // 4, fc)] = bank(4 + fc)
                 mx1(i, fc, mbanks[(i // 4, fc)])
+
+        def M2_(i0, fc):
+            mx1(i0, fc, mbanks[(i0 // 4, fc)])
+            mx1(i0 + 1, fc, mbanks[(i0 // 4, fc)])
 
         def B_(G, fc):
             mbanks[(G, fc)] = bank(4 + fc % 4)
@@ -215,11 +236,17 @@ def tile_straight_through_weight_gradient_s9_kernel(
                 in_=x_grp[G][:, c0 : c0 + n, :].rearrange("p c j -> p (c j)"),
             )
 
-        def A_(ct):
-            nc.scalar.activation(out=w_sb[:, ct, :], in_=w_sb[:, ct, :], func=ACT.Abs)
+        def A_(a):
+            s = w_sb[:, 2 * a : 2 * a + 2, :]
+            nc.scalar.activation(out=s, in_=s, func=ACT.Abs)
 
-        def K_(ct):
-            nc.vector.tensor_tensor(out=mask[:, ct, :], in0=w_sb[:, ct, :], in1=r_bc[:], op=OP.is_le)
+        def K_(a):
+            nc.vector.tensor_tensor(
+                out=mask[:, 2 * a : 2 * a + 2, :],
+                in0=w_sb[:, 2 * a : 2 * a + 2, :],
+                in1=r_bc[:].unsqueeze(1).to_broadcast([P, 2, F]),
+                op=OP.is_le,
+            )
 
         obanks = {}
         counter = {"n": 0}
@@ -239,52 +266,74 @@ def tile_straight_through_weight_gradient_s9_kernel(
                     stop=(G == TG - 1),
                 )
 
-        def O_(ct, h, eng="v"):
+        def O_(ct, h, eng="v", pieces=1):
             res = outs.tile([P, 512], F32, name="res")
-            m = mask[:, ct, h * 512 : (h + 1) * 512]
-            if eng == "v":
-                nc.vector.tensor_tensor(out=res[:], in0=obanks[(ct, h)][:], in1=m, op=OP.mult)
-            else:
-                nc.scalar.copy(out=res[:], in_=obanks[(ct, h)][:])
-                nc.gpsimd.tensor_tensor(out=res[:], in0=res[:], in1=m, op=OP.mult)
-            nc.sync.dma_start(out=out[ct * P : (ct + 1) * P, h * 512 : (h + 1) * 512], in_=res[:])
+            n = 512 // pieces
+            for k in range(pieces):
+                sl = slice(k * n, (k + 1) * n)
+                m = mask[:, ct, h * 512 + k * n : h * 512 + (k + 1) * n]
+                if eng == "v":
+                    nc.vector.tensor_tensor(out=res[:, sl], in0=obanks[(ct, h)][:, sl], in1=m, op=OP.mult)
+                else:
+                    nc.scalar.copy(out=res[:, sl], in_=obanks[(ct, h)][:, sl])
+                    nc.gpsimd.tensor_tensor(out=res[:, sl], in0=res[:, sl], in1=m, op=OP.mult)
+            return res
 
-        T_(0); C_(0); T_(1); C_(1); Q_(0); T_(2); C_(2); Q_(1); T_(3); C_(3); Q_(2)
+        def D_(ct, h, res, pieces=1):
+            n = 512 // pieces
+            for k in range(pieces):
+                nc.sync.dma_start(
+                    out=out[ct * P : (ct + 1) * P, h * 512 + k * n : h * 512 + (k + 1) * n],
+                    in_=res[:, k * n : (k + 1) * n],
+                )
+
+        T_(0); C_(0)
+        T_(1); C_(1); Q_(0)
+        T_(2); C_(2); VT_(); Q_(1); T_(3); C_(3); Q_(2); VB_(0, gain_bc);
         M_(0); Q_(3)
-        M_(1); T_(4); C_(4)
-        T_(5); C_(5); Q_(4)
-        M_(2); CL_(0, 0); CL_(0, 1); CL_(0, 2); CL_(0, 3); Q_(5)
-        I_(0, 0, 256, "s"); I_(0, 256, 256, "s")
-        M_(3); G_(0, 0); G_(0, 1); G_(0, 2); QE_(0, 0, 256); G_(0, 3)
-        B_(0, 4); I_(0, 512, 256, "s"); QE_(0, 256, 256)
+        M_(1); CL_(0, 0); CL_(0, 1); CL_(0, 2); CL_(0, 3)
+        I_(0, 512, 256, "s"); I_(0, 768, 256, "s")
+        I_(0, 0, 256, "v"); I_(0, 256, 256, "v")
+        for fc in range(4):
+            M2_(2, fc)
+            G_(0, fc)
+        T_(4); C_(4); T_(5); C_(5); Q_(4); QE_(0, 0, 512); Q_(5)
+        B_(0, 4); CL_(1, 0); CL_(1, 1); CL_(1, 2); CL_(1, 3)
+        I_(1, 0, 256, "s")
         B_(0, 5); G_(0, 4)
-        T_(6); C_(6); T_(7); C_(7); G_(0, 5); Q_(6); QE_(0, 512, 256)
-        I_(0, 768, 256, "s")
-        B_(0, 6); CL_(1, 0); CL_(1, 1); CL_(1, 2); CL_(1, 3); Q_(7)
-        I_(1, 0, 256, "s"); I_(1, 256, 256, "s")
-        B_(0, 7); G_(0, 6); QX_(0, 0, 512); G_(0, 7); QX_(0, 512, 512)
-        I_(1, 512, 256, "s"); I_(1, 768, 256, "s")
-        QE_(0, 768, 256)
-        for fc in range(8):
-            B_(1, fc)
-            A_(fc)
-            if fc > 0:
-                G_(1, fc - 1)
-            if fc == 3:
-                QX_(1, 0, 512)
-            if fc == 5:
-                QX_(1, 512, 512)
-            if fc in (3, 5, 7):
-                QE_(1, 128 * (fc - 3), 256)
-            if fc > 3:
-                K_(fc - 4)
-        G_(1, 7)
-        K_(4)
-        QE_(1, 768, 256)
-        order = [(0, 0), (1, 0), (2, 0), (0, 1), (1, 1), (2, 1), (3, 0), (3, 1), (4, 0), (4, 1), (5, 0), (5, 1),
-                 (6, 0), (6, 1), (7, 0), (7, 1)]
-        for n, (ct, h) in enumerate(order):
+        T_(6); C_(6); T_(7); C_(7); G_(0, 5); Q_(6)
+        I_(1, 256, 256, "s"); I_(1, 512, 256, "s"); I_(1, 768, 256, "s")
+        B_(0, 6); Q_(7); QX_(0, 0, 512)
+        B_(0, 7); G_(0, 6); QX_(0, 512, 512); G_(0, 7)
+        order = [(c, h) for h in range(2) for c in range(6)] + [(6, 0), (7, 0), (6, 1), (7, 1)]
+        late = []
+
+        def step2(n):
+            ct, h = order[n]
             S2_(ct, h)
-            if n in (2, 5, 8):
-                K_(n // 3 + 5)
-            O_(ct, h, "s" if n in (4, 7, 10, 12) else "v")
+            by_g = n in BYG
+            res = O_(ct, h, "s" if by_g else "v", 2 if n == 15 else 1)
+            if by_g:
+                late.append((ct, h, res))
+            else:
+                D_(ct, h, res, 2 if n == 15 else 1)
+                if n in (9, 12, 13, 14):
+                    D_(*late.pop(0))
+
+        BYG = (4, 6, 8, 10)
+        A_(0); A_(1); A_(2); A_(3)
+        B_(1, 0); QE_(0, 512, 512)
+        B_(1, 1); G_(1, 0)
+        B_(1, 2); G_(1, 1); QX_(1, 0, 512)
+        B_(1, 3); G_(1, 2); K_(0)
+        B_(1, 4); G_(1, 3); QX_(1, 512, 512); QE_(1, 0, 512)
+        B_(1, 5); G_(1, 4); K_(1)
+        step2(0)
+        B_(1, 6); G_(1, 5)
+        step2(1)
+        B_(1, 7); G_(1, 6); QE_(1, 512, 256)
+        step2(2); G_(1, 7)
+        step2(3); QE_(1, 768, 256)
+        K_(2); K_(3)
+        for n in range(4, 16):
+            step2(n)

@@ -33,8 +33,6 @@ def tile_straight_through_weight_gradient_s9_kernel(
         psum = ctx.enter_context(tc.psum_pool(name="psum", bufs=1))
         ctx.enter_context(tc.manual_schedule())
 
-        vrow = keep.tile([P, P], BF16)
-        nc.vector.memset(vrow[:], 0.0)
         vs = keep.tile([P, KG, F], U8, align_bytes=64)
         nc.vector.memset(vs[:].rearrange("p g n -> p (g n)").bitcast(I32), 0)
         warm = keep.tile([P, 1], F32)
@@ -43,8 +41,6 @@ def tile_straight_through_weight_gradient_s9_kernel(
         nc.scalar.activation(out=warm2[:], in_=warm[:], func=ACT.Abs)
         ident = keep.tile([P, P], F32)
         make_identity(nc, ident[:])
-        ident_bf = keep.tile([P, P], BF16)
-        nc.vector.tensor_copy(out=ident_bf[:], in_=ident[:])
         lo_sb = keep.tile([P, TG, 4], BF16)
         hi_sb = keep.tile([P, TG, 4], BF16)
         nc.gpsimd.dma_start(out=lo_sb[:], in_=lo.rearrange("(g p j) -> p g j", p=P, j=4))
@@ -80,30 +76,29 @@ def tile_straight_through_weight_gradient_s9_kernel(
         def load_vw(h):
             nc.sync.dma_start(out=vw[h][:], in_=vw_v[:, :, h * F : (h + 1) * F])
 
-        def load_x(g):
-            for a in range(2):
+        def load_x(g, a):
+            if True:
                 nc.sync.dma_start(out=x_sb[g][:, 2 * a : 2 * a + 2, :], in_=x_v[g, :, 2 * a : 2 * a + 2, :])
 
         def load_w(a):
             nc.sync.dma_start(out=w_sb[:, 2 * a : 2 * a + 2, :], in_=w_v[:, 2 * a : 2 * a + 2, :])
 
-        load_d(0, 2)
-        load_d(1)
-        nc.sync.dma_start(out=vrow[0:8, :], in_=gain.rearrange("(c p) -> c p", p=P))
-        load_d(2)
-        load_vs()
-        load_d(3)
-        load_vw(0)
-        load_x(0)
-        load_d(4)
-        load_d(5)
-        load_vw(1)
-        load_x(1)
-        load_d(6)
-        load_d(7)
-        for a in range(4):
-            load_w(a)
-        nc.sync.dma_start(out=r_bc[:], in_=r.partition_broadcast(P))
+        loads = "d0 d1 d2 d3 vs vh0 d4 d5 x0a x0b gain x1a d6 d7 vh1 x1b w0 r w1 w2 w3"
+        for word in loads.split():
+            if word == "vs":
+                load_vs()
+            elif word == "gain":
+                nc.sync.dma_start(out=gain_bc[:], in_=gain.partition_broadcast(P))
+            elif word == "r":
+                nc.sync.dma_start(out=r_bc[:], in_=r.partition_broadcast(P))
+            elif word[0] == "v":
+                load_vw(int(word[2]))
+            elif word[0] == "x":
+                load_x(int(word[1]), {"a": 0, "b": 1}[word[2]])
+            elif word[0] == "w":
+                load_w(int(word[1]))
+            else:
+                load_d(int(word[1]), 2 if word == "d0" else 1)
 
         d_codes = [keep.tile([P, 512], U32, name=f"d_codes{i}", align_bytes=64) for i in range(8)]
         d_scales = [keep.tile([P, 512], U8, name=f"d_scales{i}", align_bytes=64) for i in range(8)]
@@ -122,9 +117,9 @@ def tile_straight_through_weight_gradient_s9_kernel(
         mbanks = {}
         d_grp = {}
 
-        def T_(i):
+        def T_(i, b):
             words = d_sb[i][:].bitcast(F32)
-            for b in range(2):
+            if True:
                 ps = bank((i % 2) * 2 + b)
                 tbanks[(i, b)] = ps
                 for s in range(2):
@@ -135,27 +130,14 @@ def tile_straight_through_weight_gradient_s9_kernel(
                             ps[:, q * P : (q + 1) * P], words[:, k0 + u : k0 + 256 : 2], ident[:]
                         )
 
-        v_cols = keep.tile([P, 8], BF16)
-
-        def VT_():
-            ps = psum.tile([P, 1024], BF16, name="bank4v", tag="bank4")
-            nc.tensor.transpose(ps[:, 0:P], vrow[:], ident_bf[:])
-            nc.vector.tensor_copy(out=v_cols[:], in_=ps[:, 0:8])
-
-        def VB_(n, dst):
-            ps = psum.tile([P, 1024], BF16, name=f"bank{5 + n}v", tag=f"bank{5 + n}")
-            for c in range(8):
-                nc.tensor.transpose(
-                    ps[:, c * P : (c + 1) * P], v_cols[:, 8 * n + c : 8 * n + c + 1].to_broadcast([P, P]), ident_bf[:]
-                )
-            nc.scalar.copy(out=dst[:], in_=ps[:])
-
-        def C_(i):
-            grp = stage.tile([P, KG, P, 4], BF16, name="d_grp", align_bytes=64)
-            d_grp[i] = grp
+        def C_(i, b):
+            if b == 0:
+                grp = stage.tile([P, KG, P, 4], BF16, name="d_grp", align_bytes=64)
+                d_grp[i] = grp
+            grp = d_grp[i]
             gw = grp[:].rearrange("p g r t -> p (g r t)").bitcast(F32)
             gw = gw.rearrange("p (g r u) -> p g r u", g=KG, u=2)
-            for b in range(2):
+            if True:
                 nc.scalar.copy(
                     out=gw[:, 2 * b : 2 * b + 2, :, :],
                     in_=tbanks[(i, b)][:].rearrange("p (s u r) -> p s r u", s=2, u=2),
@@ -181,15 +163,10 @@ def tile_straight_through_weight_gradient_s9_kernel(
                     stop=(g == KG - 1),
                 )
 
-        def M_(i):
-            for fc in range(4):
-                if i % 4 == 0:
-                    mbanks[(i // 4, fc)] = bank(4 + fc)
-                mx1(i, fc, mbanks[(i // 4, fc)])
-
-        def M2_(i0, fc):
-            mx1(i0, fc, mbanks[(i0 // 4, fc)])
-            mx1(i0 + 1, fc, mbanks[(i0 // 4, fc)])
+        def M_(i, fc):
+            if i == 0:
+                mbanks[(0, fc)] = bank(4 + fc)
+            mx1(i, fc, mbanks[(0, fc)])
 
         def B_(G, fc):
             mbanks[(G, fc)] = bank(4 + fc % 4)
@@ -287,53 +264,60 @@ def tile_straight_through_weight_gradient_s9_kernel(
                     in_=res[:, k * n : (k + 1) * n],
                 )
 
-        T_(0); C_(0)
-        T_(1); C_(1); Q_(0)
-        T_(2); C_(2); VT_(); Q_(1); T_(3); C_(3); Q_(2); VB_(0, gain_bc);
-        M_(0); Q_(3)
-        M_(1); CL_(0, 0); CL_(0, 1); CL_(0, 2); CL_(0, 3)
-        I_(0, 512, 256, "s"); I_(0, 768, 256, "s")
-        I_(0, 0, 256, "v"); I_(0, 256, 256, "v")
-        for fc in range(4):
-            M2_(2, fc)
-            G_(0, fc)
-        T_(4); C_(4); T_(5); C_(5); Q_(4); QE_(0, 0, 512); Q_(5)
-        B_(0, 4); CL_(1, 0); CL_(1, 1); CL_(1, 2); CL_(1, 3)
-        I_(1, 0, 256, "s")
-        B_(0, 5); G_(0, 4)
-        T_(6); C_(6); T_(7); C_(7); G_(0, 5); Q_(6)
-        I_(1, 256, 256, "s"); I_(1, 512, 256, "s"); I_(1, 768, 256, "s")
-        B_(0, 6); Q_(7); QX_(0, 0, 512)
-        B_(0, 7); G_(0, 6); QX_(0, 512, 512); G_(0, 7)
-        order = [(c, h) for h in range(2) for c in range(6)] + [(6, 0), (7, 0), (6, 1), (7, 1)]
-        late = []
+        res = {}
 
-        def step2(n):
-            ct, h = order[n]
-            S2_(ct, h)
-            by_g = n in BYG
-            res = O_(ct, h, "s" if by_g else "v", 2 if n == 15 else 1)
-            if by_g:
-                late.append((ct, h, res))
+        def P_(ct, h):
+            res[(ct, h)] = O_(ct, h, "s")
+
+        def E_(G, k):
+            if G == 0 or k == 0:
+                QE_(G, 512 * k, 512)
             else:
-                D_(ct, h, res, 2 if n == 15 else 1)
-                if n in (9, 12, 13, 14):
-                    D_(*late.pop(0))
+                QE_(1, 256 + 256 * k, 256)
 
-        BYG = (4, 6, 8, 10)
-        A_(0); A_(1); A_(2); A_(3)
-        B_(1, 0); QE_(0, 512, 512)
-        B_(1, 1); G_(1, 0)
-        B_(1, 2); G_(1, 1); QX_(1, 0, 512)
-        B_(1, 3); G_(1, 2); K_(0)
-        B_(1, 4); G_(1, 3); QX_(1, 512, 512); QE_(1, 0, 512)
-        B_(1, 5); G_(1, 4); K_(1)
-        step2(0)
-        B_(1, 6); G_(1, 5)
-        step2(1)
-        B_(1, 7); G_(1, 6); QE_(1, 512, 256)
-        step2(2); G_(1, 7)
-        step2(3); QE_(1, 768, 256)
-        K_(2); K_(3)
-        for n in range(4, 16):
-            step2(n)
+        steps = """T00 C00 T01 C01 Q0 T10 C10 T11 C11 Q1 T20 C20 T21 C21 Q2 T30 C30 T31 C31 Q3 L00 L01 L02 L03
+        M00 M01 M02 M03 T40 C40 T41 C41 T50 C50 T51 C51 I01 I02 I03 M10 M20 M30 G00 Q4 I00 Q5 M11 M21
+        M31 G01 L10 L11 M12 M22 M32 G02 M13 M23 M33 G03 X00 X01 E00 L12 L13 T60 C60 T61 C61 Q6 T70
+        C70 T71 C71 A0 A1 I10 I11 A2 I12 I13 A3 Q7 B04 G04 B05 G05 K0 B06 G06 B07 G07 K1 E01 B10 G10
+        B11 G11 B12 G12 B13 G13 X10 E10 B14 G14 K2 B15 G15 X11 B16 G16 S00 O00 D00 B17 G17 E11 E12
+        S10 O10 K3 D10 S20 O20 D20 S30 O30 D30 S40 P40 O40 S50 P50 O50 S01 O01 D01 D40 S11 O11 D11
+        S21 O21 D21 D50 S31 O31 D31 S41 O41 D41 S51 O51 D51 S60 P60 O60 S70 O70 D70 S61 O61 D61 D60
+        S71 O71 D71"""
+        last = "71"
+        on_v = set("I00".split())
+        for word in steps.split():
+            kind, a = word[0], int(word[1])
+            b = int(word[2]) if len(word) > 2 else 0
+            if kind == "T":
+                T_(a, b)
+            elif kind == "C":
+                C_(a, b)
+            elif kind == "Q":
+                Q_(a)
+            elif kind == "M":
+                M_(a, b)
+            elif kind == "B":
+                B_(a, b)
+            elif kind == "G":
+                G_(a, b)
+            elif kind == "E":
+                E_(a, b)
+            elif kind == "L":
+                CL_(a, b)
+            elif kind == "I":
+                I_(a, 256 * b, 256, "v" if word in on_v else "s")
+            elif kind == "X":
+                QX_(a, 512 * b, 512)
+            elif kind == "A":
+                A_(a)
+            elif kind == "K":
+                K_(a)
+            elif kind == "S":
+                S2_(a, b)
+            elif kind == "P":
+                P_(a, b)
+            elif kind == "O":
+                if (a, b) not in res:
+                    res[(a, b)] = O_(a, b, "v", 2 if word[1:] == last else 1)
+            else:
+                D_(a, b, res[(a, b)], 2 if word[1:] == last else 1)

@@ -83,7 +83,7 @@ def tile_straight_through_weight_gradient_s9_kernel(
         def load_w(a):
             nc.sync.dma_start(out=w_sb[:, 2 * a : 2 * a + 2, :], in_=w_v[:, 2 * a : 2 * a + 2, :])
 
-        loads = "d0 d1 d2 d3 vs vh0 d4 d5 x0a x0b gain x1a d6 d7 vh1 x1b w0 r w1 w2 w3"
+        loads = "d0 d1 d2 vs d3 vh0 d4 x0a d5 x0b gain d6 d7 vh1 w0 x1a w1 x1b r w2 w3"
         for word in loads.split():
             if word == "vs":
                 load_vs()
@@ -202,7 +202,10 @@ def tile_straight_through_weight_gradient_s9_kernel(
             o = x_grp[G][:, c0 : c0 + n, :]
             i = x_sb[G][:, :, c0 : c0 + n].rearrange("p j c -> p c j")
             if eng == "s":
-                nc.scalar.copy(out=o, in_=i)
+                nc.scalar.copy(
+                    out=o.rearrange("p (c i) j -> p c j i", i=4),
+                    in_=x_sb[G][:, :, c0 : c0 + n].rearrange("p j (c i) -> p c j i", i=4),
+                )
             else:
                 nc.vector.tensor_copy(out=o, in_=i)
 
@@ -276,15 +279,15 @@ def tile_straight_through_weight_gradient_s9_kernel(
                 QE_(1, 256 + 256 * k, 256)
 
         steps = """T00 C00 T01 C01 Q0 T10 C10 T11 C11 Q1 T20 C20 T21 C21 Q2 T30 C30 T31 C31 Q3 L00 L01 L02 L03
-        M00 M01 M02 M03 T40 C40 T41 C41 T50 C50 T51 C51 I01 I02 I03 M10 M20 M30 G00 Q4 I00 Q5 M11 M21
-        M31 G01 L10 L11 M12 M22 M32 G02 M13 M23 M33 G03 X00 X01 E00 L12 L13 T60 C60 T61 C61 Q6 T70
-        C70 T71 C71 A0 A1 I10 I11 A2 I12 I13 A3 Q7 B04 G04 B05 G05 K0 B06 G06 B07 G07 K1 E01 B10 G10
-        B11 G11 B12 G12 B13 G13 X10 E10 B14 G14 K2 B15 G15 X11 B16 G16 S00 O00 D00 B17 G17 E11 E12
-        S10 O10 K3 D10 S20 O20 D20 S30 O30 D30 S40 P40 O40 S50 P50 O50 S01 O01 D01 D40 S11 O11 D11
-        S21 O21 D21 D50 S31 O31 D31 S41 O41 D41 S51 O51 D51 S60 P60 O60 S70 O70 D70 S61 O61 D61 D60
-        S71 O71 D71"""
+        M00 M01 T40 C40 T41 C41 I00 Q4 I02 I03 X01 M02 M03 M10 M20 M30 G00 T50 C50 T51 C51 I01 Q5 M11
+        M21 M31 G01 M12 M22 M32 G02 T60 C60 T61 C61 M13 M23 M33 G03 X00 Q6 E00 L10 L11 T70 C70 T71
+        C71 A0 A1 B04 G04 Q7 B05 G05 L12 L13 B06 I12 I13 I10 I11 A2 G06 B07 G07 K0 E01 B10 G10 K1 X11
+        B11 G11 B12 G12 B13 G13 X10 E10 B14 G14 B15 G15 B16 G16 K2 S00 P00 A3 O00 B17 G17 S10 O10 E11
+        E12 D10 D00 S20 P20 O20 S30 O30 D30 S40 O40 D40 D20 S50 P50 O50 S01 O01 D01 S11 O11 K3 D11
+        S21 O21 D21 D50 S31 O31 D31 S41 P41 O41 S51 O51 D51 D41 S60 O60 D60 S70 O70 D70 S61 P61 O61
+        D61 S71 O71 D71"""
         last = "71"
-        on_v = set("I00".split())
+        on_v = set("I02 I03".split())
         for word in steps.split():
             kind, a = word[0], int(word[1])
             b = int(word[2]) if len(word) > 2 else 0

@@ -43,8 +43,6 @@ def tile_straight_through_weight_gradient_s9_kernel(
         make_identity(nc, ident[:])
         lo_sb = keep.tile([P, TG, 4], BF16)
         hi_sb = keep.tile([P, TG, 4], BF16)
-        nc.gpsimd.dma_start(out=lo_sb[:], in_=lo.rearrange("(g p j) -> p g j", p=P, j=4))
-        nc.gpsimd.dma_start(out=hi_sb[:], in_=hi.rearrange("(g p j) -> p g j", p=P, j=4))
 
         delta_v = delta.rearrange("(g m t) k -> g t m k", m=P, t=4)
         x_v = x.rearrange("(g p j) c -> g p j c", p=P, j=4)
@@ -83,7 +81,9 @@ def tile_straight_through_weight_gradient_s9_kernel(
         def load_w(a):
             nc.sync.dma_start(out=w_sb[:, 2 * a : 2 * a + 2, :], in_=w_v[:, 2 * a : 2 * a + 2, :])
 
-        loads = "d0 d1 d2 vs d3 vh0 d4 x0a d5 x0b gain d6 d7 vh1 w0 x1a w1 x1b r w2 w3"
+        nc.gpsimd.dma_start(out=lo_sb[:], in_=lo.rearrange("(g p j) -> p g j", p=P, j=4))
+        nc.gpsimd.dma_start(out=hi_sb[:], in_=hi.rearrange("(g p j) -> p g j", p=P, j=4))
+        loads = "d0 d1 d2 vs d3 vh0 d4 x0a d5 x0b gain d6 vh1 d7 x1a x1b w0 r w1 w2 w3"
         for word in loads.split():
             if word == "vs":
                 load_vs()
@@ -116,6 +116,15 @@ def tile_straight_through_weight_gradient_s9_kernel(
         tbanks = {}
         mbanks = {}
         d_grp = {}
+        d_perm = {}
+
+        def R_(i):
+            perm = keep.tile([P, O // 2], F32, name=f"d_perm{i}")
+            nc.vector.tensor_copy(
+                out=perm[:].rearrange("p (g u w) -> p g u w", g=KG, u=2),
+                in_=d_sb[i][:].bitcast(F32).rearrange("p (g w u) -> p g u w", g=KG, u=2),
+            )
+            d_perm[i] = perm
 
         def T_(i, b):
             words = d_sb[i][:].bitcast(F32)
@@ -126,9 +135,11 @@ def tile_straight_through_weight_gradient_s9_kernel(
                     for u in range(2):
                         k0 = 256 * (2 * b + s)
                         q = 2 * s + u
-                        nc.tensor.transpose(
-                            ps[:, q * P : (q + 1) * P], words[:, k0 + u : k0 + 256 : 2], ident[:]
-                        )
+                        if i in d_perm:
+                            src = d_perm[i][:, k0 + u * P : k0 + (u + 1) * P]
+                        else:
+                            src = words[:, k0 + u : k0 + 256 : 2]
+                        nc.tensor.transpose(ps[:, q * P : (q + 1) * P], src, ident[:])
 
         def C_(i, b):
             if b == 0:
@@ -218,7 +229,13 @@ def tile_straight_through_weight_gradient_s9_kernel(
 
         def A_(a):
             s = w_sb[:, 2 * a : 2 * a + 2, :]
-            nc.scalar.activation(out=s, in_=s, func=ACT.Abs)
+            if a == 1:
+                bits = s.rearrange("p c f -> p (c f)").bitcast(I32)
+                nc.vector.tensor_scalar(
+                    out=bits, in0=bits, scalar1=0x7FFF7FFF, scalar2=None, op0=OP.bitwise_and
+                )
+            else:
+                nc.scalar.activation(out=s, in_=s, func=ACT.Abs)
 
         def K_(a):
             nc.vector.tensor_tensor(
@@ -278,16 +295,16 @@ def tile_straight_through_weight_gradient_s9_kernel(
             else:
                 QE_(1, 256 + 256 * k, 256)
 
-        steps = """T00 C00 T01 C01 Q0 T10 C10 T11 C11 Q1 T20 C20 T21 C21 Q2 T30 C30 T31 C31 Q3 L00 L01 L02 L03
-        M00 M01 T40 C40 T41 C41 I00 Q4 I02 I03 X01 M02 M03 M10 M20 M30 G00 T50 C50 T51 C51 I01 Q5 M11
-        M21 M31 G01 M12 M22 M32 G02 T60 C60 T61 C61 M13 M23 M33 G03 X00 Q6 E00 L10 L11 T70 C70 T71
-        C71 A0 A1 B04 G04 Q7 B05 G05 L12 L13 B06 I12 I13 I10 I11 A2 G06 B07 G07 K0 E01 B10 G10 K1 X11
-        B11 G11 B12 G12 B13 G13 X10 E10 B14 G14 B15 G15 B16 G16 K2 S00 P00 A3 O00 B17 G17 S10 O10 E11
-        E12 D10 D00 S20 P20 O20 S30 O30 D30 S40 O40 D40 D20 S50 P50 O50 S01 O01 D01 S11 O11 K3 D11
-        S21 O21 D21 D50 S31 O31 D31 S41 P41 O41 S51 O51 D51 D41 S60 O60 D60 S70 O70 D70 S61 P61 O61
-        D61 S71 O71 D71"""
+        steps = """T00 C00 T01 C01 Q0 T10 C10 T11 C11 Q1 T20 C20 T21 C21 Q2 R4 T30 C30 T31 C31 Q3 L00 L01 R5 M00
+        M01 M02 M03 T40 C40 T41 C41 Q4 L02 L03 M10 I01 M20 M30 G00 M11 M21 M31 G01 I00 M12 M22 M32
+        G02 M13 M23 M33 G03 X00 T50 C50 T51 C51 Q5 E00 T60 C60 T61 C61 I02 B04 G04 Q6 L10 L11 L12 L13
+        T70 C70 T71 C71 I03 A0 I10 I11 I12 I13 A2 A3 B05 G05 Q7 X01 B06 G06 A1 B07 G07 K0 K1 B10 G10
+        E01 B11 G11 X10 B12 G12 B13 G13 B14 G14 E10 B15 G15 X11 E11 K2 B16 G16 S00 O00 D00 S10 P10
+        O10 B17 G17 S20 O20 E12 D20 S30 P30 O30 S40 O40 D40 D10 S50 O50 D50 S01 O01 D01 S11 O11 K3
+        D11 D30 S21 P21 O21 S31 O31 D31 S41 O41 D41 D21 S51 O51 D51 S60 O60 D60 S70 O70 D70 S61 P61
+        O61 D61 S71 O71 D71"""
         last = "71"
-        on_v = set("I02 I03".split())
+        on_v = set("I00".split())
         for word in steps.split():
             kind, a = word[0], int(word[1])
             b = int(word[2]) if len(word) > 2 else 0
@@ -295,6 +312,8 @@ def tile_straight_through_weight_gradient_s9_kernel(
                 T_(a, b)
             elif kind == "C":
                 C_(a, b)
+            elif kind == "R":
+                R_(a)
             elif kind == "Q":
                 Q_(a)
             elif kind == "M":

from contextlib import ExitStack

import concourse.mybir as mybir
from concourse.masks import make_identity

T, O, F, C = 1024, 2048, 1024, 1024
FLOPS = 2 * T * O * F + 2 * T * F * C

F32 = mybir.dt.float32
BF16 = mybir.dt.bfloat16
I32 = mybir.dt.int32
U32 = mybir.dt.uint32
U8 = mybir.dt.uint8
E4M3 = mybir.dt.float8_e4m3fn_x4
E5M2 = mybir.dt.float8_e5m2_x4
E2M1 = mybir.dt.float4_e2m1fn_x4
OP = mybir.AluOpType
ACT = mybir.ActivationFunctionType

P = 128
KG = O // 512
TG = T // 512


def tile_straight_through_weight_gradient_s9_kernel(
    tc, delta, v_words, v_scales, gain, x, lo, hi, w, r, out
):
    nc = tc.nc
    with ExitStack() as ctx:
        keep = ctx.enter_context(tc.tile_pool(name="keep", bufs=1))
        stage = ctx.enter_context(tc.tile_pool(name="stage", bufs=3))
        outs = ctx.enter_context(tc.tile_pool(name="outs", bufs=16))
        psum = ctx.enter_context(tc.psum_pool(name="psum", bufs=1))
        ctx.enter_context(tc.manual_schedule())

        vs = keep.tile([P, KG, F], U8, align_bytes=64)
        nc.vector.memset(vs[:].rearrange("p g n -> p (g n)").bitcast(I32), 0)
        warm = keep.tile([P, 1], F32)
        nc.vector.memset(warm[:], 0.0)
        warm2 = keep.tile([P, 1], F32)
        nc.scalar.activation(out=warm2[:], in_=warm[:], func=ACT.Abs)
        ident = keep.tile([P, P], F32)
        make_identity(nc, ident[:])
        lo_sb = keep.tile([P, TG, 4], BF16)
        hi_sb = keep.tile([P, TG, 4], BF16)

        delta_v = delta.rearrange("(g m t) k -> g t m k", m=P, t=4)
        x_v = x.rearrange("(g p j) c -> g p j c", p=P, j=4)
        w_v = w.rearrange("(ct p) f -> p ct f", p=P)
        vw_v = v_words.rearrange("g p b -> p g b")
        vs_v = v_scales.rearrange("g q n -> q g n").bitcast(I32)

        d_sb = [keep.tile([P, O], BF16, name=f"d_sb{i}") for i in range(8)]
        vw = [keep.tile([P, KG, F], U8, name=f"vw{h}", align_bytes=64) for h in range(2)]
        gain_bc = keep.tile([P, F], BF16)
        r_bc = keep.tile([P, F], BF16)
        x_sb = [keep.tile([P, 4, C], BF16, name=f"x_sb{g}") for g in range(TG)]
        w_sb = keep.tile([P, 8, F], BF16)

        def load_d(i, pieces=1):
            n = O // pieces
            for k in range(pieces):
                nc.sync.dma_start(
                    out=d_sb[i][:, k * n : (k + 1) * n],
                    in_=delta_v[i // 4, i % 4, :, k * n : (k + 1) * n],
                )

        def load_vs():
            for q in range(4):
                nc.sync.dma_start(
                    out=vs[32 * q : 32 * q + 4, :, :].bitcast(I32), in_=vs_v[4 * q : 4 * q + 4, :, :]
                )

        def load_vw(h):
            nc.sync.dma_start(out=vw[h][:], in_=vw_v[:, :, h * F : (h + 1) * F])

        def load_x(g, a):
            if True:
                nc.sync.dma_start(out=x_sb[g][:, 2 * a : 2 * a + 2, :], in_=x_v[g, :, 2 * a : 2 * a + 2, :])

        def load_w(a):
            nc.sync.dma_start(out=w_sb[:, 2 * a : 2 * a + 2, :], in_=w_v[:, 2 * a : 2 * a + 2, :])

        nc.gpsimd.dma_start(out=lo_sb[:], in_=lo.rearrange("(g p j) -> p g j", p=P, j=4))
        nc.gpsimd.dma_start(out=hi_sb[:], in_=hi.rearrange("(g p j) -> p g j", p=P, j=4))
        loads = "d0 d1 d2 vs d3 vh0 d4 x0a d5 x0b gain d6 vh1 d7 x1a x1b w0 r w1 w2 w3"
        for word in loads.split():
            if word == "vs":
                load_vs()
            elif word == "gain":
                nc.sync.dma_start(out=gain_bc[:], in_=gain.partition_broadcast(P))
            elif word == "r":
                nc.sync.dma_start(out=r_bc[:], in_=r.partition_broadcast(P))
            elif word[0] == "v":
                load_vw(int(word[2]))
            elif word[0] == "x":
                load_x(int(word[1]), {"a": 0, "b": 1}[word[2]])
            elif word[0] == "w":
                load_w(int(word[1]))
            else:
                load_d(int(word[1]), 2 if word == "d0" else 1)

        d_codes = [keep.tile([P, 512], U32, name=f"d_codes{i}", align_bytes=64) for i in range(8)]
        d_scales = [keep.tile([P, 512], U8, name=f"d_scales{i}", align_bytes=64) for i in range(8)]
        x_grp = [keep.tile([P, C, 4], BF16, name=f"x_grp{g}", align_bytes=64) for g in range(TG)]
        x_codes = [keep.tile([P, C], U32, name=f"x_codes{g}", align_bytes=64) for g in range(TG)]
        x_scales = [keep.tile([P, C], U8, name=f"x_scales{g}", align_bytes=64) for g in range(TG)]
        e_grp = [keep.tile([P, F, 4], BF16, name=f"e_grp{g}", align_bytes=64) for g in range(TG)]
        e_codes = [keep.tile([P, F], U32, name=f"e_codes{g}", align_bytes=64) for g in range(TG)]
        e_scales = [keep.tile([P, F], U8, name=f"e_scales{g}", align_bytes=64) for g in range(TG)]
        mask = keep.tile([P, 8, F], BF16)

        def bank(n):
            return psum.tile([P, 512], F32, name=f"bank{n}", tag=f"bank{n}")

        tbanks = {}
        mbanks = {}
        d_grp = {}
        d_perm = {}

        def R_(i):
            perm = keep.tile([P, O // 2], F32, name=f"d_perm{i}")
            nc.vector.tensor_copy(
                out=perm[:].rearrange("p (g u w) -> p g u w", g=KG, u=2),
                in_=d_sb[i][:].bitcast(F32).rearrange("p (g w u) -> p g u w", g=KG, u=2),
            )
            d_perm[i] = perm

        def T_(i, b):
            words = d_sb[i][:].bitcast(F32)
            if True:
                ps = bank((i % 2) * 2 + b)
                tbanks[(i, b)] = ps
                for s in range(2):
                    for u in range(2):
                        k0 = 256 * (2 * b + s)
                        q = 2 * s + u
                        if i in d_perm:
                            src = d_perm[i][:, k0 + u * P : k0 + (u + 1) * P]
                        else:
                            src = words[:, k0 + u : k0 + 256 : 2]
                        nc.tensor.transpose(ps[:, q * P : (q + 1) * P], src, ident[:])

        def C_(i, b):
            if b == 0:
                grp = stage.tile([P, KG, P, 4], BF16, name="d_grp", align_bytes=64)
                d_grp[i] = grp
            grp = d_grp[i]
            gw = grp[:].rearrange("p g r t -> p (g r t)").bitcast(F32)
            gw = gw.rearrange("p (g r u) -> p g r u", g=KG, u=2)
            if True:
                nc.scalar.copy(
                    out=gw[:, 2 * b : 2 * b + 2, :, :],
                    in_=tbanks[(i, b)][:].rearrange("p (s u r) -> p s r u", s=2, u=2),
                )

        def Q_(i):
            nc.vector.quantize_mx(
                out=d_codes[i][:].bitcast(E4M3),
                scales=d_scales[i][:],
                in_=d_grp[i][:].rearrange("p g r t -> p (g r t)"),
            )

        def mx1(i, fc, ps):
            t = i % 4
            for g in range(KG):
                nc.tensor.matmul_mx(
                    out=ps[:, t * P : (t + 1) * P],
                    lhsT=d_codes[i][:, g * P : (g + 1) * P].bitcast(E4M3),
                    lhsT_scale=d_scales[i][:, g * P : (g + 1) * P],
                    rhs=vw[fc // 4][:, g, 256 * (fc % 4) : 256 * (fc % 4) + 256].bitcast(E2M1),
                    rhs_scale=vs[:, g, P * fc : P * fc + P],
                    start=(g == 0),
                    stop=(g == KG - 1),
                )

        def M_(i, fc):
            if i == 0:
                mbanks[(0, fc)] = bank(4 + fc)
            mx1(i, fc, mbanks[(0, fc)])

        def B_(G, fc):
            mbanks[(G, fc)] = bank(4 + fc % 4)
            for t in range(4):
                mx1(4 * G + t, fc, mbanks[(G, fc)])

        def G_(G, fc):
            nc.vector.tensor_tensor(
                out=e_grp[G][:, fc * P : (fc + 1) * P, :],
                in0=mbanks[(G, fc)][:].rearrange("p (t n) -> p n t", t=4),
                in1=gain_bc[:, fc * P : (fc + 1) * P].unsqueeze(2).to_broadcast([P, P, 4]),
                op=OP.mult,
            )

        def QE_(G, f0, n):
            nc.vector.quantize_mx(
                out=e_codes[G][:, f0 : f0 + n].bitcast(E5M2),
                scales=e_scales[G][:, f0 : f0 + n],
                in_=e_grp[G][:, f0 : f0 + n, :].rearrange("p n t -> p (n t)"),
            )

        def CL_(G, j):
            nc.vector.tensor_scalar(
                out=x_sb[G][:, j, :],
                in0=x_sb[G][:, j, :],
                scalar1=lo_sb[:, G, j : j + 1],
                scalar2=hi_sb[:, G, j : j + 1],
                op0=OP.max,
                op1=OP.min,
            )

        def I_(G, c0, n, eng):
            o = x_grp[G][:, c0 : c0 + n, :]
            i = x_sb[G][:, :, c0 : c0 + n].rearrange("p j c -> p c j")
            if eng == "s":
                nc.scalar.copy(
                    out=o.rearrange("p (c i) j -> p c j i", i=4),
                    in_=x_sb[G][:, :, c0 : c0 + n].rearrange("p j (c i) -> p c j i", i=4),
                )
            else:
                nc.vector.tensor_copy(out=o, in_=i)

        def QX_(G, c0, n):
            nc.vector.quantize_mx(
                out=x_codes[G][:, c0 : c0 + n].bitcast(E4M3),
                scales=x_scales[G][:, c0 : c0 + n],
                in_=x_grp[G][:, c0 : c0 + n, :].rearrange("p c j -> p (c j)"),
            )

        def A_(a):
            s = w_sb[:, 2 * a : 2 * a + 2, :]
            if a == 1:
                bits = s.rearrange("p c f -> p (c f)").bitcast(I32)
                nc.vector.tensor_scalar(
                    out=bits, in0=bits, scalar1=0x7FFF7FFF, scalar2=None, op0=OP.bitwise_and
                )
            else:
                nc.scalar.activation(out=s, in_=s, func=ACT.Abs)

        def K_(a):
            nc.vector.tensor_tensor(
                out=mask[:, 2 * a : 2 * a + 2, :],
                in0=w_sb[:, 2 * a : 2 * a + 2, :],
                in1=r_bc[:].unsqueeze(1).to_broadcast([P, 2, F]),
                op=OP.is_le,
            )

        obanks = {}
        counter = {"n": 0}

        def S2_(ct, h):
            ps = bank(counter["n"] % 8)
            counter["n"] += 1
            obanks[(ct, h)] = ps
            for G in range(TG):
                nc.tensor.matmul_mx(
                    out=ps[:],
                    lhsT=x_codes[G][:, ct * P : (ct + 1) * P].bitcast(E4M3),
                    lhsT_scale=x_scales[G][:, ct * P : (ct + 1) * P],
                    rhs=e_codes[G][:, h * 512 : (h + 1) * 512].bitcast(E5M2),
                    rhs_scale=e_scales[G][:, h * 512 : (h + 1) * 512],
                    start=(G == 0),
                    stop=(G == TG - 1),
                )

        def O_(ct, h, eng="v", pieces=1):
            res = outs.tile([P, 512], F32, name="res")
            n = 512 // pieces
            for k in range(pieces):
                sl = slice(k * n, (k + 1) * n)
                m = mask[:, ct, h * 512 + k * n : h * 512 + (k + 1) * n]
                if eng == "v":
                    nc.vector.tensor_tensor(out=res[:, sl], in0=obanks[(ct, h)][:, sl], in1=m, op=OP.mult)
                else:
                    nc.scalar.copy(out=res[:, sl], in_=obanks[(ct, h)][:, sl])
                    nc.gpsimd.tensor_tensor(out=res[:, sl], in0=res[:, sl], in1=m, op=OP.mult)
            return res

        def D_(ct, h, res, pieces=1):
            n = 512 // pieces
            for k in range(pieces):
                nc.sync.dma_start(
                    out=out[ct * P : (ct + 1) * P, h * 512 + k * n : h * 512 + (k + 1) * n],
                    in_=res[:, k * n : (k + 1) * n],
                )

        res = {}

        def P_(ct, h):
            res[(ct, h)] = O_(ct, h, "s")

        def E_(G, k):
            if G == 0 or k == 0:
                QE_(G, 512 * k, 512)
            else:
                QE_(1, 256 + 256 * k, 256)

        steps = """T00 C00 T01 C01 Q0 T10 C10 T11 C11 Q1 T20 C20 T21 C21 Q2 R4 T30 C30 T31 C31 Q3 L00 L01 R5 M00
        M01 M02 M03 T40 C40 T41 C41 Q4 L02 L03 M10 I01 M20 M30 G00 M11 M21 M31 G01 I00 M12 M22 M32
        G02 M13 M23 M33 G03 X00 T50 C50 T51 C51 Q5 E00 T60 C60 T61 C61 I02 B04 G04 Q6 L10 L11 L12 L13
        T70 C70 T71 C71 I03 A0 I10 I11 I12 I13 A2 A3 B05 G05 Q7 X01 B06 G06 A1 B07 G07 K0 K1 B10 G10
        E01 B11 G11 X10 B12 G12 B13 G13 B14 G14 E10 B15 G15 X11 E11 K2 B16 G16 S00 O00 D00 S10 P10
        O10 B17 G17 S20 O20 E12 D20 S30 P30 O30 S40 O40 D40 D10 S50 O50 D50 S01 O01 D01 S11 O11 K3
        D11 D30 S21 P21 O21 S31 O31 D31 S41 O41 D41 D21 S51 O51 D51 S60 O60 D60 S70 O70 D70 S61 P61
        O61 D61 S71 O71 D71"""
        last = "71"
        on_v = set("I00".split())
        for word in steps.split():
            kind, a = word[0], int(word[1])
            b = int(word[2]) if len(word) > 2 else 0
            if kind == "T":
                T_(a, b)
            elif kind == "C":
                C_(a, b)
            elif kind == "R":
                R_(a)
            elif kind == "Q":
                Q_(a)
            elif kind == "M":
                M_(a, b)
            elif kind == "B":
                B_(a, b)
            elif kind == "G":
                G_(a, b)
            elif kind == "E":
                E_(a, b)
            elif kind == "L":
                CL_(a, b)
            elif kind == "I":
                I_(a, 256 * b, 256, "v" if word in on_v else "s")
            elif kind == "X":
                QX_(a, 512 * b, 512)
            elif kind == "A":
                A_(a)
            elif kind == "K":
                K_(a)
            elif kind == "S":
                S2_(a, b)
            elif kind == "P":
                P_(a, b)
            elif kind == "O":
                if (a, b) not in res:
                    res[(a, b)] = O_(a, b, "v", 2 if word[1:] == last else 1)
            else:
                D_(a, b, res[(a, b)], 2 if word[1:] == last else 1)
